import numpy as np
import ml_dtypes


def mxq(x, axis, fmt="e4m3"):
    dtype, down = {"e4m3": (ml_dtypes.float8_e4m3fn, 7), "e5m2": (ml_dtypes.float8_e5m2, 14)}[fmt]
    v = np.moveaxis(np.asarray(x, np.float32).astype(ml_dtypes.bfloat16).astype(np.float64), axis, -1)
    blocks = v.reshape(v.shape[:-1] + (-1, 32))
    amax = np.abs(blocks).max(-1, keepdims=True)
    byte = np.maximum(np.where(amax > 0, np.frexp(amax)[1] - 1 + 127, 0) - down, 1)
    scale = np.exp2(byte - 127.0)
    codes = (blocks / scale).astype(np.float32).astype(dtype).astype(np.float64)
    return np.moveaxis((codes * scale).reshape(v.shape), -1, axis)


WIDE = False


def mx_kscale(k):
    if not WIDE:
        return np.ones(k)
    levels = np.array([10, -10, 5, -5, 0])
    if k % 512:
        return np.exp2(np.random.permutation(np.resize(levels, k // 32))).repeat(32)
    a = np.empty((k // 512, 16))
    for p in range(k // 512):
        a[p, :8] = np.random.permutation(np.resize(levels, 8))
        for g in range(8):
            far = levels[np.abs(levels - a[p, g]) >= 10]
            a[p, g + 8] = far[np.random.randint(len(far))]
    return np.exp2(a.ravel()).repeat(32)


BF16 = ml_dtypes.bfloat16


def bf(x):
    return np.asarray(x, np.float32).astype(BF16)


def f64(x):
    return np.asarray(x).astype(np.float64)


B, D = 6144, 512


def sigmoid(v):
    return 1.0 / (1.0 + np.exp(-v))


def draw0():
    s = mx_kscale(D)
    t = mx_kscale(D)
    return {"x": bf(np.random.standard_normal((B, D)) * s[None, :]),
            "wg": bf(np.random.standard_normal((D, D)) / np.sqrt(D) / s[:, None]),
            "wc1": bf(np.random.standard_normal((D, D)) / np.sqrt(D) / s[:, None]),
            "gm": bf((1.0 + 0.1 * np.random.standard_normal(D)) * t / s),
            "wc2": bf(np.random.standard_normal((D, D)) / np.sqrt(D) / t[:, None])}


def core(x, wg, wc1, gm, wc2):
    x = f64(x)
    xq = mxq(x, 1, "e4m3")
    xg = x * sigmoid(xq @ mxq(f64(wg), 0, "e4m3"))
    f1 = xq @ mxq(f64(wc1), 0, "e4m3")
    c1 = xg * f1 + x
    u = c1 * f64(gm)[None, :]
    f2 = mxq(u, 1, "e4m3") @ mxq(f64(wc2), 0, "e4m3")
    return xg * f2 + c1


def e4m3fn_bytes(y):
    return np.clip(np.asarray(y, np.float64), -448.0, 448.0).astype(np.float32).astype(ml_dtypes.float8_e4m3fn).view(np.uint8)


def e4m3fn_values(b):
    return np.asarray(b, np.uint8).view(ml_dtypes.float8_e4m3fn).astype(np.float64)


def setup_inputs():
    d = draw0()
    x0 = np.asarray(d['wg']).astype(np.float64)
    s = (np.max(np.abs(x0), axis=(1,), keepdims=True) / 448.0).astype(np.float32)
    out = {}
    for k, v in d.items():
        if k == 'wg':
            out['wg_bytes'] = e4m3fn_bytes(x0 / s.astype(np.float64))
            out['wg_scale'] = s
        else:
            out[k] = v
    return out


def reference(x, wg_bytes, wg_scale, wc1, gm, wc2):
    return core(x, e4m3fn_values(wg_bytes) * wg_scale.astype(np.float64), wc1, gm, wc2)

@@ -1,0 +1,273 @@
+from contextlib import ExitStack
+
+import concourse.mybir as mybir
+from concourse.masks import make_identity
+
+B, D = 6144, 512
+P = 128
+T = 4
+A = 4
+N = A * P
+G = B // N
+FLOPS = 3 * 2 * B * D * D
+
+F32 = mybir.dt.float32
+BF16 = mybir.dt.bfloat16
+U32 = mybir.dt.uint32
+U8 = mybir.dt.uint8
+FP8 = mybir.dt.float8_e4m3fn
+FP8X4 = mybir.dt.float8_e4m3fn_x4
+ACT = mybir.ActivationFunctionType
+ALU = mybir.AluOpType
+
+
+def tile_gateddeepcrosstwolayer_t_kernel(tc, x, wg_bytes, wg_scale, wc1, gm, wc2, out):
+    nc = tc.nc
+    x_groups = x.rearrange("(g p a) d -> g p (a d)", p=P, a=A)
+    out_groups = out.rearrange("(g p a) d -> g p (a d)", p=P, a=A)
+
+    with ExitStack() as ctx:
+        const = ctx.enter_context(tc.tile_pool(name="const", bufs=1))
+        work = ctx.enter_context(tc.tile_pool(name="work", bufs=2))
+        psum = ctx.enter_context(tc.psum_pool(name="psum", bufs=1))
+
+        ident = const.tile([P, P], F32)
+        make_identity(nc, ident[:])
+        ctx.enter_context(tc.manual_schedule())
+
+        gm_raw = const.tile([P, T], BF16)
+        scale = const.tile([P, T], F32)
+        wg_raw = const.tile([P, T, D], U8)
+        wc1_raw = const.tile([P, T, D], BF16)
+        wc2_raw = const.tile([P, T, D], BF16)
+        x_sb = {}
+
+        def load_x(g):
+            x_tile = const.tile([P, A * D], BF16, tag="x", bufs=G)
+            nc.sync.dma_start(out=x_tile[:], in_=x_groups[g])
+            x_sb[g] = x_tile
+
+        nc.sync.dma_start(out=scale[:], in_=wg_scale.rearrange("(p t) o -> p (t o)", t=T))
+        nc.sync.dma_start(out=wg_raw[:], in_=wg_bytes.rearrange("(p t) n -> p t n", t=T))
+        load_x(0)
+        nc.sync.dma_start(out=wc1_raw[:], in_=wc1.rearrange("(p t) n -> p t n", t=T))
+        nc.sync.dma_start(out=gm_raw[:], in_=gm.rearrange("(p t) -> p t", t=T))
+        load_x(1)
+        nc.sync.dma_start(out=wc2_raw[:], in_=wc2.rearrange("(p t) n -> p t n", t=T))
+        for g in range(2, G):
+            load_x(g)
+
+        warm = const.tile([P, 1], F32)
+        nc.vector.memset(warm[:], 0.0)
+        nc.scalar.activation(out=warm[:], in_=warm[:], func=ACT.Sigmoid)
+
+        grouped, x_codes, x_scales = {}, {}, {}
+        xt = {}
+        f1, gate_psum, sig, h, hg = {}, {}, {}, {}, {}
+        u_codes, u_scales, h2, hp2, ot = {}, {}, {}, {}, {}
+
+        def x_transpose(g):
+            words = x_sb[g][:].bitcast(F32)
+            for half in range(2):
+                bank = psum.tile([P, 2, 2, P], F32, tag="tr", bufs=3)
+                for i in range(2):
+                    a = 2 * half + i
+                    for u in range(2):
+                        nc.tensor.transpose(bank[:, i, u, :], words[:, 256 * a + u : 256 * (a + 1) : 2], ident[:])
+                xt[g, half] = bank
+
+        def x_group_copy(g):
+            tile = work.tile([P, N * T], BF16, tag="grouped", bufs=4, align_bytes=64)
+            words = tile[:].bitcast(F32)
+            for half in range(2):
+                nc.scalar.copy(
+                    out=words[:, 512 * half : 512 * (half + 1)].rearrange("p (i r u) -> p i r u", i=2, u=2),
+                    in_=xt.pop((g, half))[:].rearrange("p i u r -> p i r u"),
+                )
+            grouped[g] = tile
+
+        def x_quantize(g):
+            codes = work.tile([P, N], U32, tag="xc", bufs=3, align_bytes=64)
+            scales = work.tile([P, N], U8, tag="xs", bufs=3, align_bytes=64)
+            nc.vector.quantize_mx(out=codes[:].bitcast(FP8X4), scales=scales[:], in_=grouped[g][:])
+            x_codes[g], x_scales[g] = codes, scales
+
+        def mm(bank, w, t, codes, scales, start, stop):
+            w_codes, w_scales = w
+            cols = slice(P * t, P * (t + 1))
+            nc.tensor.matmul_mx(
+                out=bank[:],
+                lhsT=w_codes[:, cols].bitcast(FP8X4),
+                lhsT_scale=w_scales[:, cols],
+                rhs=codes[:].bitcast(FP8X4),
+                rhs_scale=scales[:],
+                start=start,
+                stop=stop,
+            )
+
+        def mm_gate(g, t):
+            bank = psum.tile([P, N], F32, tag="g", bufs=2)
+            mm(bank, wg_q, t, x_codes[g], x_scales[g], True, True)
+            gate_psum[g, t] = bank
+
+        def mm_f1(g, t):
+            bank = psum.tile([P, N], F32, tag="f", bufs=3)
+            mm(bank, wc1_q, t, x_codes[g], x_scales[g], True, True)
+            f1[g, t] = bank
+
+        def mm_f12(g, t):
+            bank = psum.tile([P, N], F32, tag="f", bufs=3)
+            mm(bank, wc1_q, t, x_codes[g], x_scales[g], True, False)
+            mm(bank, wc2_q, t, u_codes[g], u_scales[g], False, True)
+            f1[g, t] = bank
+
+        def sigmoid(g, t):
+            tile = work.tile([P, N], F32, tag="sig", bufs=10)
+            nc.scalar.activation(out=tile[:], in_=gate_psum.pop((g, t))[:], func=ACT.Sigmoid)
+            sig[g, t] = tile
+
+        def h_mul(g, t):
+            tile = work.tile([P, N], F32, tag="h", bufs=4)
+            nc.vector.tensor_tensor(out=tile[:], in0=f1.pop((g, t))[:], in1=sig[g, t][:], op=ALU.mult)
+            h[g, t] = tile
+
+        def h_gain(g, t):
+            if t == 0:
+                hg[g] = work.tile([P, T, N], F32, tag="hg", bufs=2, name="hg")
+            nc.scalar.activation(
+                out=hg[g][:, t, :], in_=h.pop((g, t))[:], func=ACT.Identity, scale=gain[:, t : t + 1], bias=gain[:, t : t + 1]
+            )
+
+        def u_mul(g):
+            tile = work.tile([P, N, T], BF16, tag="u", bufs=2, align_bytes=64)
+            nc.vector.tensor_tensor(
+                out=tile[:],
+                in0=hg.pop(g)[:].rearrange("p t n -> p n t"),
+                in1=grouped[g][:].rearrange("p (n t) -> p n t", t=T),
+                op=ALU.mult,
+            )
+            return tile
+
+        def u_quantize(g, tile):
+            codes = work.tile([P, N], U32, tag="uc", bufs=2, align_bytes=64)
+            scales = work.tile([P, N], U8, tag="us", bufs=2, align_bytes=64)
+            nc.vector.quantize_mx(
+                out=codes[:].bitcast(FP8X4), scales=scales[:], in_=tile[:].rearrange("p n t -> p (n t)")
+            )
+            u_codes[g], u_scales[g] = codes, scales
+
+        def h2_mul(g, t):
+            tile = work.tile([P, N], F32, tag="h2", bufs=8)
+            nc.vector.tensor_tensor(out=tile[:], in0=f1.pop((g, t))[:], in1=sig.pop((g, t))[:], op=ALU.mult)
+            h2[g, t] = tile
+
+        def out_transpose(g, a):
+            bank = psum.tile([P, T, P], F32, tag="tr", bufs=3)
+            for t in range(T):
+                nc.tensor.transpose(bank[:, t, :], h2[g, t][:, P * a : P * (a + 1)], ident[:])
+            ot[g, a] = bank
+
+        def out_evacuate(g, a):
+            if a == 0:
+                hp2[g] = work.tile([P, A, D], F32, tag="hp2", bufs=2, name="hp2")
+            nc.scalar.activation(
+                out=hp2[g][:, a, :].rearrange("r (p t) -> r p t", t=T),
+                in_=ot.pop((g, a))[:].rearrange("r t p -> r p t"),
+                func=ACT.Copy,
+                bias=1.0,
+            )
+
+        def out_mul(g):
+            tile = work.tile([P, A * D], F32, tag="out", bufs=2)
+            nc.gpsimd.tensor_tensor(
+                out=tile[:], in0=hp2.pop(g)[:].rearrange("p a d -> p (a d)"), in1=x_sb[g][:], op=ALU.mult
+            )
+            nc.sync.dma_start(out=out_groups[g], in_=tile[:])
+
+        def out_direct(g, a):
+            tile = work.tile([P, D], F32, tag="last", bufs=4)
+            nc.vector.scalar_tensor_tensor(
+                out=tile[:].rearrange("r (p t) -> r p t", t=T),
+                in0=ot.pop((g, a))[:].rearrange("r t p -> r p t"),
+                scalar=1.0,
+                in1=x_sb[g][:, D * a : D * (a + 1)].rearrange("r (p t) -> r p t", t=T),
+                op0=ALU.add,
+                op1=ALU.mult,
+            )
+            nc.sync.dma_start(out=out_groups[g][:, D * a : D * (a + 1)], in_=tile[:])
+
+        def weight_group(raw, name):
+            tile = const.tile([P, T * P * T], BF16, tag="wgrouped", bufs=2, align_bytes=64, name=name)
+            nc.vector.tensor_copy(
+                out=tile[:].rearrange("p (t m j) -> p t m j", t=T, j=T),
+                in_=raw[:].rearrange("p j (m t) -> p t m j", t=T),
+            )
+            return tile
+
+        def weight_quantize(tile, name):
+            codes = const.tile([P, D], U32, align_bytes=64, name=name + "_codes")
+            scales = const.tile([P, D], U8, align_bytes=64, name=name + "_scales")
+            nc.vector.quantize_mx(out=codes[:].bitcast(FP8X4), scales=scales[:], in_=tile[:])
+            return codes, scales
+
+        x_transpose(0)
+        wg_wide = const.tile([P, T, D], BF16)
+        for j in range(T):
+            nc.scalar.activation(
+                out=wg_wide[:, j, :], in_=wg_raw[:, j, :].bitcast(FP8), func=ACT.Copy, scale=scale[:, j : j + 1]
+            )
+        x_group_copy(0)
+        x_transpose(1)
+        wg_grouped = weight_group(wg_wide, "wg_grouped")
+        x_quantize(0)
+        wg_q = weight_quantize(wg_grouped, "wg")
+        mm_gate(0, 0)
+        sigmoid(0, 0)
+        wc1_grouped = weight_group(wc1_raw, "wc1_grouped")
+        gain = const.tile([P, T], F32)
+        nc.vector.tensor_copy(out=gain[:], in_=gm_raw[:])
+        wc1_q = weight_quantize(wc1_grouped, "wc1")
+        x_group_copy(1)
+
+        for s in range(G + 1):
+            first = s if s < G else None
+            second = s - 1 if s > 0 else None
+            for t in range(T):
+                if first is not None:
+                    mm_f1(first, t)
+                    if t + 1 < T:
+                        mm_gate(first, t + 1)
+                        sigmoid(first, t + 1)
+                    h_mul(first, t)
+                if second is not None:
+                    mm_f12(second, t)
+                    h2_mul(second, t)
+                if first is not None:
+                    h_gain(first, t)
+            if s == 0:
+                wc2_grouped = weight_group(wc2_raw, "wc2_grouped")
+            if s + 1 < G:
+                x_quantize(s + 1)
+            if s == 0:
+                wc2_q = weight_quantize(wc2_grouped, "wc2")
+            if s + 2 < G:
+                x_transpose(s + 2)
+                x_group_copy(s + 2)
+            if first is not None:
+                u_tile = u_mul(first)
+                u_quantize(first, u_tile)
+            if second is not None and s < G:
+                for a in range(A - 1):
+                    out_transpose(second, a)
+                    out_evacuate(second, a)
+                out_transpose(second, A - 1)
+            if s + 1 < G:
+                mm_gate(s + 1, 0)
+                sigmoid(s + 1, 0)
+            if second is not None and s < G:
+                out_evacuate(second, A - 1)
+                out_mul(second)
+            if s == G:
+                for a in range(A):
+                    out_transpose(second, a)
+                    out_direct(second, a)

@@ -9,6 +9,52 @@ T = 4
 A = 4
 N = A * P
 G = B // N
+ORDER = (
+    ("h_mul", 0, 0),
+    ("mm_gate", 0, 2),
+    ("h_gain", 0, 0),
+    ("mm_f12", -1, 0),
+    ("h2_mul", -1, 0),
+    ("mm_f1", 0, 1),
+    ("h_mul", 0, 1),
+    ("sigmoid", 0, 2),
+    ("mm_f12", -1, 1),
+    ("h2_mul", -1, 1),
+    ("mm_gate", 0, 3),
+    ("h_gain", 0, 1),
+    ("mm_f1", 0, 2),
+    ("h_mul", 0, 2),
+    ("sigmoid", 0, 3),
+    ("mm_f12", -1, 2),
+    ("mm_f1", 0, 3),
+    ("h_mul", 0, 3),
+    ("h_gain", 0, 2),
+    ("h2_mul", -1, 2),
+    ("mm_f12", -1, 3),
+    ("h_gain", 0, 3),
+    ("h2_mul", -1, 3),
+    ("x_transpose", 2, 0),
+    ("x_transpose", 2, 1),
+    ("mm_gate", 1, 0),
+    ("mm_gate", 1, 1),
+    ("x_group_copy", 2, 0),
+    ("x_group_copy", 2, 1),
+    ("out_transpose", -1, 0),
+    ("out_transpose", -1, 1),
+    ("mm_f1", 1, 0),
+    ("out_transpose", -1, 2),
+    ("sigmoid", 1, 0),
+    ("out_evacuate", -1, 0),
+    ("out_transpose", -1, 3),
+    ("out_evacuate", -1, 1),
+    ("out_evacuate", -1, 2),
+    ("out_evacuate", -1, 3),
+    ("sigmoid", 1, 1),
+    ("u_mul", 0),
+    ("x_quantize", 2),
+    ("u_quantize", 0),
+    ("out_mul", -1),
+)
 FLOPS = 3 * 2 * B * D * D
 
 F32 = mybir.dt.float32
@@ -47,8 +93,8 @@ def tile_gateddeepcrosstwolayer_t_kernel(tc, x, wg_bytes, wg_scale, wc1, gm, wc2
             nc.sync.dma_start(out=x_tile[:], in_=x_groups[g])
             x_sb[g] = x_tile
 
-        nc.sync.dma_start(out=scale[:], in_=wg_scale.rearrange("(p t) o -> p (t o)", t=T))
         nc.sync.dma_start(out=wg_raw[:], in_=wg_bytes.rearrange("(p t) n -> p t n", t=T))
+        nc.sync.dma_start(out=scale[:], in_=wg_scale.rearrange("(p t) o -> p (t o)", t=T))
         load_x(0)
         nc.sync.dma_start(out=wc1_raw[:], in_=wc1.rearrange("(p t) n -> p t n", t=T))
         nc.sync.dma_start(out=gm_raw[:], in_=gm.rearrange("(p t) -> p t", t=T))
@@ -64,11 +110,11 @@ def tile_gateddeepcrosstwolayer_t_kernel(tc, x, wg_bytes, wg_scale, wc1, gm, wc2
         grouped, x_codes, x_scales = {}, {}, {}
         xt = {}
         f1, gate_psum, sig, h, hg = {}, {}, {}, {}, {}
-        u_codes, u_scales, h2, hp2, ot = {}, {}, {}, {}, {}
+        u, u_codes, u_scales, h2, hp2, ot = {}, {}, {}, {}, {}, {}
 
-        def x_transpose(g):
+        def x_transpose(g, half):
             words = x_sb[g][:].bitcast(F32)
-            for half in range(2):
+            if True:
                 bank = psum.tile([P, 2, 2, P], F32, tag="tr", bufs=3)
                 for i in range(2):
                     a = 2 * half + i
@@ -76,15 +122,15 @@ def tile_gateddeepcrosstwolayer_t_kernel(tc, x, wg_bytes, wg_scale, wc1, gm, wc2
                         nc.tensor.transpose(bank[:, i, u, :], words[:, 256 * a + u : 256 * (a + 1) : 2], ident[:])
                 xt[g, half] = bank
 
-        def x_group_copy(g):
-            tile = work.tile([P, N * T], BF16, tag="grouped", bufs=4, align_bytes=64)
-            words = tile[:].bitcast(F32)
-            for half in range(2):
+        def x_group_copy(g, half):
+            if half == 0:
+                grouped[g] = work.tile([P, N * T], BF16, tag="grouped", bufs=5, align_bytes=64, name="grouped")
+            words = grouped[g][:].bitcast(F32)
+            if True:
                 nc.scalar.copy(
                     out=words[:, 512 * half : 512 * (half + 1)].rearrange("p (i r u) -> p i r u", i=2, u=2),
                     in_=xt.pop((g, half))[:].rearrange("p i u r -> p i r u"),
                 )
-            grouped[g] = tile
 
         def x_quantize(g):
             codes = work.tile([P, N], U32, tag="xc", bufs=3, align_bytes=64)
@@ -139,20 +185,21 @@ def tile_gateddeepcrosstwolayer_t_kernel(tc, x, wg_bytes, wg_scale, wc1, gm, wc2
             )
 
         def u_mul(g):
-            tile = work.tile([P, N, T], BF16, tag="u", bufs=2, align_bytes=64)
+            tile = work.tile([P, N * T], BF16, tag="u", bufs=2, align_bytes=64)
             nc.vector.tensor_tensor(
-                out=tile[:],
-                in0=hg.pop(g)[:].rearrange("p t n -> p n t"),
-                in1=grouped[g][:].rearrange("p (n t) -> p n t", t=T),
+                out=tile[:].rearrange("p (c i t) -> p c t i", i=4, t=T),
+                in0=hg.pop(g)[:].rearrange("p t (c i) -> p c t i", i=4),
+                in1=grouped[g][:].rearrange("p (c i t) -> p c t i", i=4, t=T),
                 op=ALU.mult,
             )
-            return tile
+            u[g] = tile
 
-        def u_quantize(g, tile):
+        def u_quantize(g):
+            tile = u.pop(g)
             codes = work.tile([P, N], U32, tag="uc", bufs=2, align_bytes=64)
             scales = work.tile([P, N], U8, tag="us", bufs=2, align_bytes=64)
             nc.vector.quantize_mx(
-                out=codes[:].bitcast(FP8X4), scales=scales[:], in_=tile[:].rearrange("p n t -> p (n t)")
+                out=codes[:].bitcast(FP8X4), scales=scales[:], in_=tile[:]
             )
             u_codes[g], u_scales[g] = codes, scales
 
@@ -168,6 +215,9 @@ def tile_gateddeepcrosstwolayer_t_kernel(tc, x, wg_bytes, wg_scale, wc1, gm, wc2
             ot[g, a] = bank
 
         def out_evacuate(g, a):
+            if g == G - 1:
+                out_direct(g, a)
+                return
             if a == 0:
                 hp2[g] = work.tile([P, A, D], F32, tag="hp2", bufs=2, name="hp2")
             nc.scalar.activation(
@@ -178,6 +228,8 @@ def tile_gateddeepcrosstwolayer_t_kernel(tc, x, wg_bytes, wg_scale, wc1, gm, wc2
             )
 
         def out_mul(g):
+            if g == G - 1:
+                return
             tile = work.tile([P, A * D], F32, tag="out", bufs=2)
             nc.gpsimd.tensor_tensor(
                 out=tile[:], in0=hp2.pop(g)[:].rearrange("p a d -> p (a d)"), in1=x_sb[g][:], op=ALU.mult
@@ -210,64 +262,34 @@ def tile_gateddeepcrosstwolayer_t_kernel(tc, x, wg_bytes, wg_scale, wc1, gm, wc2
             nc.vector.quantize_mx(out=codes[:].bitcast(FP8X4), scales=scales[:], in_=tile[:])
             return codes, scales
 
-        x_transpose(0)
         wg_wide = const.tile([P, T, D], BF16)
-        for j in range(T):
-            nc.scalar.activation(
-                out=wg_wide[:, j, :], in_=wg_raw[:, j, :].bitcast(FP8), func=ACT.Copy, scale=scale[:, j : j + 1]
-            )
-        x_group_copy(0)
-        x_transpose(1)
-        wg_grouped = weight_group(wg_wide, "wg_grouped")
-        x_quantize(0)
-        wg_q = weight_quantize(wg_grouped, "wg")
-        mm_gate(0, 0)
-        sigmoid(0, 0)
-        wc1_grouped = weight_group(wc1_raw, "wc1_grouped")
         gain = const.tile([P, T], F32)
-        nc.vector.tensor_copy(out=gain[:], in_=gm_raw[:])
-        wc1_q = weight_quantize(wc1_grouped, "wc1")
-        x_group_copy(1)
+        for j in range(T):
+            column = scale[:, j : j + 1]
+            codes = wg_raw[:, j, :].bitcast(FP8)
+            if j < 2:
+                nc.scalar.activation(out=wg_wide[:, j, :], in_=codes, func=ACT.Copy, scale=column)
+            else:
+                nc.vector.tensor_scalar(out=wg_wide[:, j, :], in0=codes, scalar1=column, scalar2=None, op0=ALU.mult)
+        steps = {
+            "x_transpose": x_transpose, "x_group_copy": x_group_copy, "x_quantize": x_quantize, "mm_gate": mm_gate, "mm_f1": mm_f1,
+            "sigmoid": sigmoid, "h_mul": h_mul, "h_gain": h_gain, "u_mul": u_mul, "u_quantize": u_quantize, "mm_f12": mm_f12,
+            "h2_mul": h2_mul, "out_transpose": out_transpose, "out_evacuate": out_evacuate, "out_mul": out_mul,
+        }
 
-        for s in range(G + 1):
-            first = s if s < G else None
-            second = s - 1 if s > 0 else None
-            for t in range(T):
-                if first is not None:
-                    mm_f1(first, t)
-                    if t + 1 < T:
-                        mm_gate(first, t + 1)
-                        sigmoid(first, t + 1)
-                    h_mul(first, t)
-                if second is not None:
-                    mm_f12(second, t)
-                    h2_mul(second, t)
-                if first is not None:
-                    h_gain(first, t)
-            if s == 0:
-                wc2_grouped = weight_group(wc2_raw, "wc2_grouped")
-            if s + 1 < G:
-                x_quantize(s + 1)
-            if s == 0:
-                wc2_q = weight_quantize(wc2_grouped, "wc2")
-            if s + 2 < G:
-                x_transpose(s + 2)
-                x_group_copy(s + 2)
-            if first is not None:
-                u_tile = u_mul(first)
-                u_quantize(first, u_tile)
-            if second is not None and s < G:
-                for a in range(A - 1):
-                    out_transpose(second, a)
-                    out_evacuate(second, a)
-                out_transpose(second, A - 1)
-            if s + 1 < G:
-                mm_gate(s + 1, 0)
-                sigmoid(s + 1, 0)
-            if second is not None and s < G:
-                out_evacuate(second, A - 1)
-                out_mul(second)
-            if s == G:
-                for a in range(A):
-                    out_transpose(second, a)
-                    out_direct(second, a)
+        def run_slot(s, order):
+            for step, lead, *index in order:
+                if 0 <= s + lead < G:
+                    steps[step](s + lead, *index)
+
+        wg_q = weight_quantize(weight_group(wg_wide, "wg_grouped"), "wg")
+        run_slot(-2, ORDER)
+        wc1_q = weight_quantize(weight_group(wc1_raw, "wc1_grouped"), "wc1")
+        nc.vector.tensor_copy(out=gain[:], in_=gm_raw[:])
+        run_slot(-1, ORDER)
+        cut = ORDER.index(("u_mul", 0))
+        run_slot(0, ORDER[:cut])
+        wc2_q = weight_quantize(weight_group(wc2_raw, "wc2_grouped"), "wc2")
+        run_slot(0, ORDER[cut:])
+        for s in range(1, G + 1):
+            run_slot(s, ORDER)

@@ -9,51 +9,55 @@ T = 4
 A = 4
 N = A * P
 G = B // N
+NEV = 1
 ORDER = (
+    ("sigmoid", 0, 1),
     ("h_mul", 0, 0),
+    ("h2_mul", -2, 0),
+    ("mm_f1", 0, 1),
     ("mm_gate", 0, 2),
     ("h_gain", 0, 0),
-    ("mm_f12", -1, 0),
-    ("h2_mul", -1, 0),
-    ("mm_f1", 0, 1),
-    ("h_mul", 0, 1),
     ("sigmoid", 0, 2),
-    ("mm_f12", -1, 1),
-    ("h2_mul", -1, 1),
+    ("mm_f12", -2, 1),
+    ("h_mul", 0, 1),
+    ("u_mul", -1, 2),
+    ("h2_mul", -2, 1),
+    ("mm_f1", 0, 2),
     ("mm_gate", 0, 3),
     ("h_gain", 0, 1),
-    ("mm_f1", 0, 2),
-    ("h_mul", 0, 2),
     ("sigmoid", 0, 3),
-    ("mm_f12", -1, 2),
-    ("mm_f1", 0, 3),
-    ("h_mul", 0, 3),
-    ("h_gain", 0, 2),
-    ("h2_mul", -1, 2),
-    ("mm_f12", -1, 3),
-    ("h_gain", 0, 3),
-    ("h2_mul", -1, 3),
+    ("mm_f12", -2, 2),
+    ("h_mul", 0, 2),
     ("x_transpose", 2, 0),
+    ("h2_mul", -2, 2),
+    ("u_mul", -1, 3),
+    ("mm_f1", 0, 3),
+    ("x_group_copy", 2, 0),
+    ("h_gain", 0, 2),
+    ("mm_f12", -2, 3),
+    ("h_mul", 0, 3),
     ("x_transpose", 2, 1),
+    ("h2_mul", -2, 3),
+    ("x_group_copy", 2, 1),
+    ("h_gain", 0, 3),
     ("mm_gate", 1, 0),
     ("mm_gate", 1, 1),
-    ("x_group_copy", 2, 0),
-    ("x_group_copy", 2, 1),
-    ("out_transpose", -1, 0),
-    ("out_transpose", -1, 1),
-    ("mm_f1", 1, 0),
-    ("out_transpose", -1, 2),
-    ("sigmoid", 1, 0),
-    ("out_evacuate", -1, 0),
-    ("out_transpose", -1, 3),
-    ("out_evacuate", -1, 1),
-    ("out_evacuate", -1, 2),
-    ("out_evacuate", -1, 3),
-    ("sigmoid", 1, 1),
-    ("u_mul", 0),
+    ("u_quantize", -1),
     ("x_quantize", 2),
-    ("u_quantize", 0),
-    ("out_mul", -1),
+    ("out_transpose", -2, 0),
+    ("out_transpose", -2, 1),
+    ("mm_f1", 1, 0),
+    ("out_finish", -2, 0),
+    ("out_transpose", -2, 2),
+    ("out_finish", -2, 1),
+    ("out_transpose", -2, 3),
+    ("out_finish", -2, 2),
+    ("out_finish", -2, 3),
+    ("sigmoid", 1, 0),
+    ("mm_f12", -1, 0),
+    ("out_mul", -2, 0),
+    ("u_mul", 0, 0),
+    ("u_mul", 0, 1),
 )
 FLOPS = 3 * 2 * B * D * D
 
@@ -89,9 +93,9 @@ def tile_gateddeepcrosstwolayer_t_kernel(tc, x, wg_bytes, wg_scale, wc1, gm, wc2
         x_sb = {}
 
         def load_x(g):
-            x_tile = const.tile([P, A * D], BF16, tag="x", bufs=G)
-            nc.sync.dma_start(out=x_tile[:], in_=x_groups[g])
-            x_sb[g] = x_tile
+            tile = const.tile([P, A * D], BF16, tag="x", bufs=G)
+            nc.sync.dma_start(out=tile[:], in_=x_groups[g])
+            x_sb[g] = tile
 
         nc.sync.dma_start(out=wg_raw[:], in_=wg_bytes.rearrange("(p t) n -> p t n", t=T))
         nc.sync.dma_start(out=scale[:], in_=wg_scale.rearrange("(p t) o -> p (t o)", t=T))
@@ -106,162 +110,170 @@ def tile_gateddeepcrosstwolayer_t_kernel(tc, x, wg_bytes, wg_scale, wc1, gm, wc2
         warm = const.tile([P, 1], F32)
         nc.vector.memset(warm[:], 0.0)
         nc.scalar.activation(out=warm[:], in_=warm[:], func=ACT.Sigmoid)
+        zeros = const.tile([P, N], BF16)
+        nc.gpsimd.memset(zeros[:], 0.0)
 
-        grouped, x_codes, x_scales = {}, {}, {}
-        xt = {}
-        f1, gate_psum, sig, h, hg = {}, {}, {}, {}, {}
-        u, u_codes, u_scales, h2, hp2, ot = {}, {}, {}, {}, {}, {}
+        def keep_warm(n):
+            for i in range(n):
+                bank = psum.tile([P, N], F32, tag="gate", bufs=2)
+                nc.tensor.matmul(out=bank[:], lhsT=zeros[:, :P], rhs=zeros[:], start=True, stop=True)
+
+        xt, grouped, x_q, gate, f, sig, h, hg, u, u_q, h2, ot, plus = {}, {}, {}, {}, {}, {}, {}, {}, {}, {}, {}, {}, {}
 
         def x_transpose(g, half):
             words = x_sb[g][:].bitcast(F32)
-            if True:
-                bank = psum.tile([P, 2, 2, P], F32, tag="tr", bufs=3)
-                for i in range(2):
-                    a = 2 * half + i
-                    for u in range(2):
-                        nc.tensor.transpose(bank[:, i, u, :], words[:, 256 * a + u : 256 * (a + 1) : 2], ident[:])
-                xt[g, half] = bank
+            bank = psum.tile([P, 2, 2, P], F32, tag="turn", bufs=3)
+            for i in range(2):
+                a = 2 * half + i
+                for e in range(2):
+                    nc.tensor.transpose(bank[:, i, e, :], words[:, 256 * a + e : 256 * (a + 1) : 2], ident[:])
+            xt[g, half] = bank
 
         def x_group_copy(g, half):
             if half == 0:
                 grouped[g] = work.tile([P, N * T], BF16, tag="grouped", bufs=5, align_bytes=64, name="grouped")
             words = grouped[g][:].bitcast(F32)
-            if True:
-                nc.scalar.copy(
-                    out=words[:, 512 * half : 512 * (half + 1)].rearrange("p (i r u) -> p i r u", i=2, u=2),
-                    in_=xt.pop((g, half))[:].rearrange("p i u r -> p i r u"),
-                )
+            ins = xt.pop((g, half))[:].rearrange("p i u r -> p i r u")
+            outs = words[:, N * half : N * (half + 1)].rearrange("p (i r u) -> p i r u", i=2, u=2)
+            if False:
+                nc.vector.tensor_copy(out=outs, in_=ins)
+            else:
+                nc.scalar.copy(out=outs, in_=ins)
+
+        def quantize(tile, codes, scales):
+            nc.vector.quantize_mx(out=codes[:].bitcast(FP8X4), scales=scales[:], in_=tile[:])
+            return codes, scales
 
         def x_quantize(g):
-            codes = work.tile([P, N], U32, tag="xc", bufs=3, align_bytes=64)
-            scales = work.tile([P, N], U8, tag="xs", bufs=3, align_bytes=64)
-            nc.vector.quantize_mx(out=codes[:].bitcast(FP8X4), scales=scales[:], in_=grouped[g][:])
-            x_codes[g], x_scales[g] = codes, scales
+            codes = work.tile([P, N], U32, tag="x_codes", bufs=5, align_bytes=64)
+            scales = work.tile([P, N], U8, tag="x_scales", bufs=5, align_bytes=64)
+            x_q[g] = quantize(grouped[g], codes, scales)
 
-        def mm(bank, w, t, codes, scales, start, stop):
-            w_codes, w_scales = w
+        def mm(bank, w, t, data, start, stop):
             cols = slice(P * t, P * (t + 1))
             nc.tensor.matmul_mx(
                 out=bank[:],
-                lhsT=w_codes[:, cols].bitcast(FP8X4),
-                lhsT_scale=w_scales[:, cols],
-                rhs=codes[:].bitcast(FP8X4),
-                rhs_scale=scales[:],
+                lhsT=w[0][:, cols].bitcast(FP8X4),
+                lhsT_scale=w[1][:, cols],
+                rhs=data[0][:].bitcast(FP8X4),
+                rhs_scale=data[1][:],
                 start=start,
                 stop=stop,
             )
 
         def mm_gate(g, t):
-            bank = psum.tile([P, N], F32, tag="g", bufs=2)
-            mm(bank, wg_q, t, x_codes[g], x_scales[g], True, True)
-            gate_psum[g, t] = bank
+            bank = psum.tile([P, N], F32, tag="gate", bufs=2)
+            mm(bank, wg_q, t, x_q[g], True, True)
+            gate[g, t] = bank
 
         def mm_f1(g, t):
             bank = psum.tile([P, N], F32, tag="f", bufs=3)
-            mm(bank, wc1_q, t, x_codes[g], x_scales[g], True, True)
-            f1[g, t] = bank
+            mm(bank, wc1_q, t, x_q[g], True, True)
+            f[g, t] = bank
 
         def mm_f12(g, t):
             bank = psum.tile([P, N], F32, tag="f", bufs=3)
-            mm(bank, wc1_q, t, x_codes[g], x_scales[g], True, False)
-            mm(bank, wc2_q, t, u_codes[g], u_scales[g], False, True)
-            f1[g, t] = bank
+            mm(bank, wc1_q, t, x_q[g], True, False)
+            mm(bank, wc2_q, t, u_q[g], False, True)
+            f[g, t] = bank
 
         def sigmoid(g, t):
-            tile = work.tile([P, N], F32, tag="sig", bufs=10)
-            nc.scalar.activation(out=tile[:], in_=gate_psum.pop((g, t))[:], func=ACT.Sigmoid)
+            tile = work.tile([P, N], F32, tag="sig", bufs=14)
+            nc.scalar.activation(out=tile[:], in_=gate.pop((g, t))[:], func=ACT.Sigmoid)
             sig[g, t] = tile
 
         def h_mul(g, t):
             tile = work.tile([P, N], F32, tag="h", bufs=4)
-            nc.vector.tensor_tensor(out=tile[:], in0=f1.pop((g, t))[:], in1=sig[g, t][:], op=ALU.mult)
+            nc.vector.tensor_tensor(out=tile[:], in0=f.pop((g, t))[:], in1=sig[g, t][:], op=ALU.mult)
             h[g, t] = tile
 
         def h_gain(g, t):
             if t == 0:
                 hg[g] = work.tile([P, T, N], F32, tag="hg", bufs=2, name="hg")
-            nc.scalar.activation(
-                out=hg[g][:, t, :], in_=h.pop((g, t))[:], func=ACT.Identity, scale=gain[:, t : t + 1], bias=gain[:, t : t + 1]
-            )
+            column = gain[:, t : t + 1]
+            nc.scalar.activation(out=hg[g][:, t, :], in_=h.pop((g, t))[:], func=ACT.Identity, scale=column, bias=column)
 
-        def u_mul(g):
-            tile = work.tile([P, N * T], BF16, tag="u", bufs=2, align_bytes=64)
-            nc.vector.tensor_tensor(
-                out=tile[:].rearrange("p (c i t) -> p c t i", i=4, t=T),
-                in0=hg.pop(g)[:].rearrange("p t (c i) -> p c t i", i=4),
-                in1=grouped[g][:].rearrange("p (c i t) -> p c t i", i=4, t=T),
+        def u_mul(g, a):
+            if a == 0:
+                u[g] = work.tile([P, N * T], BF16, tag="u", bufs=2, align_bytes=64, name="u")
+            cols = slice(P * T * a, P * T * (a + 1))
+            nc.gpsimd.tensor_tensor(
+                out=u[g][:, cols].rearrange("p (n t) -> p n t", t=T),
+                in0=hg[g][:, :, P * a : P * (a + 1)].rearrange("p t n -> p n t"),
+                in1=grouped[g][:, cols].rearrange("p (n t) -> p n t", t=T),
                 op=ALU.mult,
             )
-            u[g] = tile
 
         def u_quantize(g):
-            tile = u.pop(g)
-            codes = work.tile([P, N], U32, tag="uc", bufs=2, align_bytes=64)
-            scales = work.tile([P, N], U8, tag="us", bufs=2, align_bytes=64)
-            nc.vector.quantize_mx(
-                out=codes[:].bitcast(FP8X4), scales=scales[:], in_=tile[:]
-            )
-            u_codes[g], u_scales[g] = codes, scales
+            codes = work.tile([P, N], U32, tag="u_codes", bufs=3, align_bytes=64)
+            scales = work.tile([P, N], U8, tag="u_scales", bufs=3, align_bytes=64)
+            u_q[g] = quantize(u.pop(g), codes, scales)
 
         def h2_mul(g, t):
             tile = work.tile([P, N], F32, tag="h2", bufs=8)
-            nc.vector.tensor_tensor(out=tile[:], in0=f1.pop((g, t))[:], in1=sig.pop((g, t))[:], op=ALU.mult)
+            nc.vector.tensor_tensor(out=tile[:], in0=f.pop((g, t))[:], in1=sig.pop((g, t))[:], op=ALU.mult)
             h2[g, t] = tile
 
         def out_transpose(g, a):
-            bank = psum.tile([P, T, P], F32, tag="tr", bufs=3)
+            bank = psum.tile([P, T, P], F32, tag="turn", bufs=3)
             for t in range(T):
                 nc.tensor.transpose(bank[:, t, :], h2[g, t][:, P * a : P * (a + 1)], ident[:])
             ot[g, a] = bank
 
-        def out_evacuate(g, a):
-            if g == G - 1:
-                out_direct(g, a)
-                return
-            if a == 0:
-                hp2[g] = work.tile([P, A, D], F32, tag="hp2", bufs=2, name="hp2")
-            nc.scalar.activation(
-                out=hp2[g][:, a, :].rearrange("r (p t) -> r p t", t=T),
-                in_=ot.pop((g, a))[:].rearrange("r t p -> r p t"),
-                func=ACT.Copy,
-                bias=1.0,
-            )
-
-        def out_mul(g):
-            if g == G - 1:
-                return
-            tile = work.tile([P, A * D], F32, tag="out", bufs=2)
-            nc.gpsimd.tensor_tensor(
-                out=tile[:], in0=hp2.pop(g)[:].rearrange("p a d -> p (a d)"), in1=x_sb[g][:], op=ALU.mult
-            )
-            nc.sync.dma_start(out=out_groups[g], in_=tile[:])
-
-        def out_direct(g, a):
-            tile = work.tile([P, D], F32, tag="last", bufs=4)
-            nc.vector.scalar_tensor_tensor(
-                out=tile[:].rearrange("r (p t) -> r p t", t=T),
-                in0=ot.pop((g, a))[:].rearrange("r t p -> r p t"),
-                scalar=1.0,
-                in1=x_sb[g][:, D * a : D * (a + 1)].rearrange("r (p t) -> r p t", t=T),
-                op0=ALU.add,
-                op1=ALU.mult,
-            )
+        def store(g, a, tile):
             nc.sync.dma_start(out=out_groups[g][:, D * a : D * (a + 1)], in_=tile[:])
+
+        def out_finish(g, a):
+            bank = ot.pop((g, a))[:].rearrange("r t p -> r p t")
+            if a < NEV:
+                tile = work.tile([P, D], F32, tag="plus", bufs=2)
+                nc.scalar.activation(out=tile[:].rearrange("r (p t) -> r p t", t=T), in_=bank, func=ACT.Copy, bias=1.0)
+                plus[g, a] = tile
+            else:
+                tile = work.tile([P, D], F32, tag="out", bufs=8)
+                nc.vector.scalar_tensor_tensor(
+                    out=tile[:].rearrange("r (p t) -> r p t", t=T),
+                    in0=bank,
+                    scalar=1.0,
+                    in1=x_sb[g][:, D * a : D * (a + 1)].rearrange("r (p t) -> r p t", t=T),
+                    op0=ALU.add,
+                    op1=ALU.mult,
+                )
+                store(g, a, tile)
+
+        def out_mul(g, a):
+            tile = work.tile([P, D], F32, tag="gp_out", bufs=2)
+            nc.gpsimd.tensor_tensor(out=tile[:], in0=plus.pop((g, a))[:], in1=x_sb[g][:, D * a : D * (a + 1)], op=ALU.mult)
+            store(g, a, tile)
 
         def weight_group(raw, name):
             tile = const.tile([P, T * P * T], BF16, tag="wgrouped", bufs=2, align_bytes=64, name=name)
-            nc.vector.tensor_copy(
-                out=tile[:].rearrange("p (t m j) -> p t m j", t=T, j=T),
-                in_=raw[:].rearrange("p j (m t) -> p t m j", t=T),
-            )
+            dst = tile[:].rearrange("p (t m j) -> p t m j", t=T, j=T)
+            src = raw[:].rearrange("p j (m t) -> p t m j", t=T)
+            if name == "wc1" and True:
+                nc.vector.tensor_copy(out=dst[:, 0:2], in_=src[:, 0:2])
+                nc.scalar.copy(out=dst[:, 2:4], in_=src[:, 2:4])
+            else:
+                nc.vector.tensor_copy(out=dst, in_=src)
             return tile
 
         def weight_quantize(tile, name):
             codes = const.tile([P, D], U32, align_bytes=64, name=name + "_codes")
             scales = const.tile([P, D], U8, align_bytes=64, name=name + "_scales")
-            nc.vector.quantize_mx(out=codes[:].bitcast(FP8X4), scales=scales[:], in_=tile[:])
-            return codes, scales
+            return quantize(tile, codes, scales)
 
+        steps = {
+            "x_transpose": x_transpose, "x_group_copy": x_group_copy, "x_quantize": x_quantize, "mm_gate": mm_gate, "mm_f1": mm_f1,
+            "sigmoid": sigmoid, "h_mul": h_mul, "h_gain": h_gain, "u_mul": u_mul, "u_quantize": u_quantize, "mm_f12": mm_f12,
+            "h2_mul": h2_mul, "out_transpose": out_transpose, "out_finish": out_finish, "out_mul": out_mul,
+        }
+
+        def run_slot(s, order):
+            for step, lead, *index in order:
+                if 0 <= s + lead < G:
+                    steps[step](s + lead, *index)
+
+        keep_warm(6)
         wg_wide = const.tile([P, T, D], BF16)
         gain = const.tile([P, T], F32)
         for j in range(T):
@@ -271,25 +283,24 @@ def tile_gateddeepcrosstwolayer_t_kernel(tc, x, wg_bytes, wg_scale, wc1, gm, wc2
                 nc.scalar.activation(out=wg_wide[:, j, :], in_=codes, func=ACT.Copy, scale=column)
             else:
                 nc.vector.tensor_scalar(out=wg_wide[:, j, :], in0=codes, scalar1=column, scalar2=None, op0=ALU.mult)
-        steps = {
-            "x_transpose": x_transpose, "x_group_copy": x_group_copy, "x_quantize": x_quantize, "mm_gate": mm_gate, "mm_f1": mm_f1,
-            "sigmoid": sigmoid, "h_mul": h_mul, "h_gain": h_gain, "u_mul": u_mul, "u_quantize": u_quantize, "mm_f12": mm_f12,
-            "h2_mul": h2_mul, "out_transpose": out_transpose, "out_evacuate": out_evacuate, "out_mul": out_mul,
-        }
-
-        def run_slot(s, order):
-            for step, lead, *index in order:
-                if 0 <= s + lead < G:
-                    steps[step](s + lead, *index)
-
-        wg_q = weight_quantize(weight_group(wg_wide, "wg_grouped"), "wg")
+        wg_q = weight_quantize(weight_group(wg_wide, "wg"), "wg")
         run_slot(-2, ORDER)
-        wc1_q = weight_quantize(weight_group(wc1_raw, "wc1_grouped"), "wc1")
+        wc1_q = weight_quantize(weight_group(wc1_raw, "wc1"), "wc1")
         nc.vector.tensor_copy(out=gain[:], in_=gm_raw[:])
-        run_slot(-1, ORDER)
-        cut = ORDER.index(("u_mul", 0))
-        run_slot(0, ORDER[:cut])
-        wc2_q = weight_quantize(weight_group(wc2_raw, "wc2_grouped"), "wc2")
-        run_slot(0, ORDER[cut:])
-        for s in range(1, G + 1):
+        run_slot(-1, [entry for entry in ORDER if entry[1] == 1])
+        run_slot(-1, [entry for entry in ORDER if entry[0] in ("x_transpose", "x_group_copy")])
+        first = ORDER.index(("h_mul", 0, 0)) + 1
+        second = ORDER.index(("h_mul", 0, 2)) + 1
+        run_slot(0, ORDER[:first])
+        wc2_grouped = weight_group(wc2_raw, "wc2")
+        run_slot(0, ORDER[first:second])
+        x_quantize(1)
+        wc2_q = weight_quantize(wc2_grouped, "wc2")
+        run_slot(0, ORDER[second:])
+        for s in range(1, G):
             run_slot(s, ORDER)
+        late = list(ORDER)
+        late.remove(("u_quantize", -1))
+        late.insert(late.index(("mm_f12", -1, 0)), ("u_quantize", -1))
+        run_slot(G, late)
+        run_slot(G + 1, ORDER)

@@ -20,7 +20,6 @@ ORDER = (
     ("sigmoid", 0, 2),
     ("mm_f12", -2, 1),
     ("h_mul", 0, 1),
-    ("u_mul", -1, 2),
     ("h2_mul", -2, 1),
     ("mm_f1", 0, 2),
     ("mm_gate", 0, 3),
@@ -30,7 +29,6 @@ ORDER = (
     ("h_mul", 0, 2),
     ("x_transpose", 2, 0),
     ("h2_mul", -2, 2),
-    ("u_mul", -1, 3),
     ("mm_f1", 0, 3),
     ("x_group_copy", 2, 0),
     ("h_gain", 0, 2),
@@ -57,7 +55,6 @@ ORDER = (
     ("mm_f12", -1, 0),
     ("out_mul", -2, 0),
     ("u_mul", 0, 0),
-    ("u_mul", 0, 1),
 )
 FLOPS = 3 * 2 * B * D * D
 
@@ -196,11 +193,12 @@ def tile_gateddeepcrosstwolayer_t_kernel(tc, x, wg_bytes, wg_scale, wc1, gm, wc2
         def u_mul(g, a):
             if a == 0:
                 u[g] = work.tile([P, N * T], BF16, tag="u", bufs=2, align_bytes=64, name="u")
-            cols = slice(P * T * a, P * T * (a + 1))
+            width = N // 1
+            cols = slice(width * T * a, width * T * (a + 1))
             nc.gpsimd.tensor_tensor(
-                out=u[g][:, cols].rearrange("p (n t) -> p n t", t=T),
-                in0=hg[g][:, :, P * a : P * (a + 1)].rearrange("p t n -> p n t"),
-                in1=grouped[g][:, cols].rearrange("p (n t) -> p n t", t=T),
+                out=u[g][:, cols].rearrange("p (c i t) -> p c t i", i=4, t=T),
+                in0=hg[g][:, :, width * a : width * (a + 1)].rearrange("p t (c i) -> p c t i", i=4),
+                in1=grouped[g][:, cols].rearrange("p (c i t) -> p c t i", i=4, t=T),
                 op=ALU.mult,
             )
 

from contextlib import ExitStack

import concourse.mybir as mybir
from concourse.masks import make_identity

B, D = 6144, 512
P = 128
T = 4
A = 4
N = A * P
G = B // N
NEV = 1
ORDER = (
    ("sigmoid", 0, 1),
    ("h_mul", 0, 0),
    ("h2_mul", -2, 0),
    ("mm_f1", 0, 1),
    ("mm_gate", 0, 2),
    ("h_gain", 0, 0),
    ("sigmoid", 0, 2),
    ("mm_f12", -2, 1),
    ("h_mul", 0, 1),
    ("h2_mul", -2, 1),
    ("mm_f1", 0, 2),
    ("mm_gate", 0, 3),
    ("h_gain", 0, 1),
    ("sigmoid", 0, 3),
    ("mm_f12", -2, 2),
    ("h_mul", 0, 2),
    ("x_transpose", 2, 0),
    ("h2_mul", -2, 2),
    ("mm_f1", 0, 3),
    ("x_group_copy", 2, 0),
    ("h_gain", 0, 2),
    ("mm_f12", -2, 3),
    ("h_mul", 0, 3),
    ("x_transpose", 2, 1),
    ("h2_mul", -2, 3),
    ("x_group_copy", 2, 1),
    ("h_gain", 0, 3),
    ("mm_gate", 1, 0),
    ("mm_gate", 1, 1),
    ("u_quantize", -1),
    ("x_quantize", 2),
    ("out_transpose", -2, 0),
    ("out_transpose", -2, 1),
    ("mm_f1", 1, 0),
    ("out_finish", -2, 0),
    ("out_transpose", -2, 2),
    ("out_finish", -2, 1),
    ("out_transpose", -2, 3),
    ("out_finish", -2, 2),
    ("out_finish", -2, 3),
    ("sigmoid", 1, 0),
    ("mm_f12", -1, 0),
    ("out_mul", -2, 0),
    ("u_mul", 0, 0),
)
FLOPS = 3 * 2 * B * D * D

F32 = mybir.dt.float32
BF16 = mybir.dt.bfloat16
U32 = mybir.dt.uint32
U8 = mybir.dt.uint8
FP8 = mybir.dt.float8_e4m3fn
FP8X4 = mybir.dt.float8_e4m3fn_x4
ACT = mybir.ActivationFunctionType
ALU = mybir.AluOpType


def tile_gateddeepcrosstwolayer_t_kernel(tc, x, wg_bytes, wg_scale, wc1, gm, wc2, out):
    nc = tc.nc
    x_groups = x.rearrange("(g p a) d -> g p (a d)", p=P, a=A)
    out_groups = out.rearrange("(g p a) d -> g p (a d)", p=P, a=A)

    with ExitStack() as ctx:
        const = ctx.enter_context(tc.tile_pool(name="const", bufs=1))
        work = ctx.enter_context(tc.tile_pool(name="work", bufs=2))
        psum = ctx.enter_context(tc.psum_pool(name="psum", bufs=1))

        ident = const.tile([P, P], F32)
        make_identity(nc, ident[:])
        ctx.enter_context(tc.manual_schedule())

        gm_raw = const.tile([P, T], BF16)
        scale = const.tile([P, T], F32)
        wg_raw = const.tile([P, T, D], U8)
        wc1_raw = const.tile([P, T, D], BF16)
        wc2_raw = const.tile([P, T, D], BF16)
        x_sb = {}

        def load_x(g):
            tile = const.tile([P, A * D], BF16, tag="x", bufs=G)
            nc.sync.dma_start(out=tile[:], in_=x_groups[g])
            x_sb[g] = tile

        nc.sync.dma_start(out=wg_raw[:], in_=wg_bytes.rearrange("(p t) n -> p t n", t=T))
        nc.sync.dma_start(out=scale[:], in_=wg_scale.rearrange("(p t) o -> p (t o)", t=T))
        load_x(0)
        nc.sync.dma_start(out=wc1_raw[:], in_=wc1.rearrange("(p t) n -> p t n", t=T))
        nc.sync.dma_start(out=gm_raw[:], in_=gm.rearrange("(p t) -> p t", t=T))
        load_x(1)
        nc.sync.dma_start(out=wc2_raw[:], in_=wc2.rearrange("(p t) n -> p t n", t=T))
        for g in range(2, G):
            load_x(g)

        warm = const.tile([P, 1], F32)
        nc.vector.memset(warm[:], 0.0)
        nc.scalar.activation(out=warm[:], in_=warm[:], func=ACT.Sigmoid)
        zeros = const.tile([P, N], BF16)
        nc.gpsimd.memset(zeros[:], 0.0)

        def keep_warm(n):
            for i in range(n):
                bank = psum.tile([P, N], F32, tag="gate", bufs=2)
                nc.tensor.matmul(out=bank[:], lhsT=zeros[:, :P], rhs=zeros[:], start=True, stop=True)

        xt, grouped, x_q, gate, f, sig, h, hg, u, u_q, h2, ot, plus = {}, {}, {}, {}, {}, {}, {}, {}, {}, {}, {}, {}, {}

        def x_transpose(g, half):
            words = x_sb[g][:].bitcast(F32)
            bank = psum.tile([P, 2, 2, P], F32, tag="turn", bufs=3)
            for i in range(2):
                a = 2 * half + i
                for e in range(2):
                    nc.tensor.transpose(bank[:, i, e, :], words[:, 256 * a + e : 256 * (a + 1) : 2], ident[:])
            xt[g, half] = bank

        def x_group_copy(g, half):
            if half == 0:
                grouped[g] = work.tile([P, N * T], BF16, tag="grouped", bufs=5, align_bytes=64, name="grouped")
            words = grouped[g][:].bitcast(F32)
            ins = xt.pop((g, half))[:].rearrange("p i u r -> p i r u")
            outs = words[:, N * half : N * (half + 1)].rearrange("p (i r u) -> p i r u", i=2, u=2)
            if False:
                nc.vector.tensor_copy(out=outs, in_=ins)
            else:
                nc.scalar.copy(out=outs, in_=ins)

        def quantize(tile, codes, scales):
            nc.vector.quantize_mx(out=codes[:].bitcast(FP8X4), scales=scales[:], in_=tile[:])
            return codes, scales

        def x_quantize(g):
            codes = work.tile([P, N], U32, tag="x_codes", bufs=5, align_bytes=64)
            scales = work.tile([P, N], U8, tag="x_scales", bufs=5, align_bytes=64)
            x_q[g] = quantize(grouped[g], codes, scales)

        def mm(bank, w, t, data, start, stop):
            cols = slice(P * t, P * (t + 1))
            nc.tensor.matmul_mx(
                out=bank[:],
                lhsT=w[0][:, cols].bitcast(FP8X4),
                lhsT_scale=w[1][:, cols],
                rhs=data[0][:].bitcast(FP8X4),
                rhs_scale=data[1][:],
                start=start,
                stop=stop,
            )

        def mm_gate(g, t):
            bank = psum.tile([P, N], F32, tag="gate", bufs=2)
            mm(bank, wg_q, t, x_q[g], True, True)
            gate[g, t] = bank

        def mm_f1(g, t):
            bank = psum.tile([P, N], F32, tag="f", bufs=3)
            mm(bank, wc1_q, t, x_q[g], True, True)
            f[g, t] = bank

        def mm_f12(g, t):
            bank = psum.tile([P, N], F32, tag="f", bufs=3)
            mm(bank, wc1_q, t, x_q[g], True, False)
            mm(bank, wc2_q, t, u_q[g], False, True)
            f[g, t] = bank

        def sigmoid(g, t):
            tile = work.tile([P, N], F32, tag="sig", bufs=14)
            nc.scalar.activation(out=tile[:], in_=gate.pop((g, t))[:], func=ACT.Sigmoid)
            sig[g, t] = tile

        def h_mul(g, t):
            tile = work.tile([P, N], F32, tag="h", bufs=4)
            nc.vector.tensor_tensor(out=tile[:], in0=f.pop((g, t))[:], in1=sig[g, t][:], op=ALU.mult)
            h[g, t] = tile

        def h_gain(g, t):
            if t == 0:
                hg[g] = work.tile([P, T, N], F32, tag="hg", bufs=2, name="hg")
            column = gain[:, t : t + 1]
            nc.scalar.activation(out=hg[g][:, t, :], in_=h.pop((g, t))[:], func=ACT.Identity, scale=column, bias=column)

        def u_mul(g, a):
            if a == 0:
                u[g] = work.tile([P, N * T], BF16, tag="u", bufs=2, align_bytes=64, name="u")
            width = N // 1
            cols = slice(width * T * a, width * T * (a + 1))
            nc.gpsimd.tensor_tensor(
                out=u[g][:, cols].rearrange("p (c i t) -> p c t i", i=4, t=T),
                in0=hg[g][:, :, width * a : width * (a + 1)].rearrange("p t (c i) -> p c t i", i=4),
                in1=grouped[g][:, cols].rearrange("p (c i t) -> p c t i", i=4, t=T),
                op=ALU.mult,
            )

        def u_quantize(g):
            codes = work.tile([P, N], U32, tag="u_codes", bufs=3, align_bytes=64)
            scales = work.tile([P, N], U8, tag="u_scales", bufs=3, align_bytes=64)
            u_q[g] = quantize(u.pop(g), codes, scales)

        def h2_mul(g, t):
            tile = work.tile([P, N], F32, tag="h2", bufs=8)
            nc.vector.tensor_tensor(out=tile[:], in0=f.pop((g, t))[:], in1=sig.pop((g, t))[:], op=ALU.mult)
            h2[g, t] = tile

        def out_transpose(g, a):
            bank = psum.tile([P, T, P], F32, tag="turn", bufs=3)
            for t in range(T):
                nc.tensor.transpose(bank[:, t, :], h2[g, t][:, P * a : P * (a + 1)], ident[:])
            ot[g, a] = bank

        def store(g, a, tile):
            nc.sync.dma_start(out=out_groups[g][:, D * a : D * (a + 1)], in_=tile[:])

        def out_finish(g, a):
            bank = ot.pop((g, a))[:].rearrange("r t p -> r p t")
            if a < NEV:
                tile = work.tile([P, D], F32, tag="plus", bufs=2)
                nc.scalar.activation(out=tile[:].rearrange("r (p t) -> r p t", t=T), in_=bank, func=ACT.Copy, bias=1.0)
                plus[g, a] = tile
            else:
                tile = work.tile([P, D], F32, tag="out", bufs=8)
                nc.vector.scalar_tensor_tensor(
                    out=tile[:].rearrange("r (p t) -> r p t", t=T),
                    in0=bank,
                    scalar=1.0,
                    in1=x_sb[g][:, D * a : D * (a + 1)].rearrange("r (p t) -> r p t", t=T),
                    op0=ALU.add,
                    op1=ALU.mult,
                )
                store(g, a, tile)

        def out_mul(g, a):
            tile = work.tile([P, D], F32, tag="gp_out", bufs=2)
            nc.gpsimd.tensor_tensor(out=tile[:], in0=plus.pop((g, a))[:], in1=x_sb[g][:, D * a : D * (a + 1)], op=ALU.mult)
            store(g, a, tile)

        def weight_group(raw, name):
            tile = const.tile([P, T * P * T], BF16, tag="wgrouped", bufs=2, align_bytes=64, name=name)
            dst = tile[:].rearrange("p (t m j) -> p t m j", t=T, j=T)
            src = raw[:].rearrange("p j (m t) -> p t m j", t=T)
            if name == "wc1" and True:
                nc.vector.tensor_copy(out=dst[:, 0:2], in_=src[:, 0:2])
                nc.scalar.copy(out=dst[:, 2:4], in_=src[:, 2:4])
            else:
                nc.vector.tensor_copy(out=dst, in_=src)
            return tile

        def weight_quantize(tile, name):
            codes = const.tile([P, D], U32, align_bytes=64, name=name + "_codes")
            scales = const.tile([P, D], U8, align_bytes=64, name=name + "_scales")
            return quantize(tile, codes, scales)

        steps = {
            "x_transpose": x_transpose, "x_group_copy": x_group_copy, "x_quantize": x_quantize, "mm_gate": mm_gate, "mm_f1": mm_f1,
            "sigmoid": sigmoid, "h_mul": h_mul, "h_gain": h_gain, "u_mul": u_mul, "u_quantize": u_quantize, "mm_f12": mm_f12,
            "h2_mul": h2_mul, "out_transpose": out_transpose, "out_finish": out_finish, "out_mul": out_mul,
        }

        def run_slot(s, order):
            for step, lead, *index in order:
                if 0 <= s + lead < G:
                    steps[step](s + lead, *index)

        keep_warm(6)
        wg_wide = const.tile([P, T, D], BF16)
        gain = const.tile([P, T], F32)
        for j in range(T):
            column = scale[:, j : j + 1]
            codes = wg_raw[:, j, :].bitcast(FP8)
            if j < 2:
                nc.scalar.activation(out=wg_wide[:, j, :], in_=codes, func=ACT.Copy, scale=column)
            else:
                nc.vector.tensor_scalar(out=wg_wide[:, j, :], in0=codes, scalar1=column, scalar2=None, op0=ALU.mult)
        wg_q = weight_quantize(weight_group(wg_wide, "wg"), "wg")
        run_slot(-2, ORDER)
        wc1_q = weight_quantize(weight_group(wc1_raw, "wc1"), "wc1")
        nc.vector.tensor_copy(out=gain[:], in_=gm_raw[:])
        run_slot(-1, [entry for entry in ORDER if entry[1] == 1])
        run_slot(-1, [entry for entry in ORDER if entry[0] in ("x_transpose", "x_group_copy")])
        first = ORDER.index(("h_mul", 0, 0)) + 1
        second = ORDER.index(("h_mul", 0, 2)) + 1
        run_slot(0, ORDER[:first])
        wc2_grouped = weight_group(wc2_raw, "wc2")
        run_slot(0, ORDER[first:second])
        x_quantize(1)
        wc2_q = weight_quantize(wc2_grouped, "wc2")
        run_slot(0, ORDER[second:])
        for s in range(1, G):
            run_slot(s, ORDER)
        late = list(ORDER)
        late.remove(("u_quantize", -1))
        late.insert(late.index(("mm_f12", -1, 0)), ("u_quantize", -1))
        run_slot(G, late)
        run_slot(G + 1, ORDER)
